import numpy as np
import ml_dtypes


def mxq(x, axis, fmt="e4m3"):
    dtype, down = {"e4m3": (ml_dtypes.float8_e4m3fn, 7), "e5m2": (ml_dtypes.float8_e5m2, 14)}[fmt]
    v = np.moveaxis(np.asarray(x, np.float32).astype(ml_dtypes.bfloat16).astype(np.float64), axis, -1)
    blocks = v.reshape(v.shape[:-1] + (-1, 32))
    amax = np.abs(blocks).max(-1, keepdims=True)
    byte = np.maximum(np.where(amax > 0, np.frexp(amax)[1] - 1 + 127, 0) - down, 1)
    scale = np.exp2(byte - 127.0)
    codes = (blocks / scale).astype(np.float32).astype(dtype).astype(np.float64)
    return np.moveaxis((codes * scale).reshape(v.shape), -1, axis)


WIDE = False


def mx_kscale(k):
    if not WIDE:
        return np.ones(k)
    levels = np.array([10, -10, 5, -5, 0])
    if k % 512:
        return np.exp2(np.random.permutation(np.resize(levels, k // 32))).repeat(32)
    a = np.empty((k // 512, 16))
    for p in range(k // 512):
        a[p, :8] = np.random.permutation(np.resize(levels, 8))
        for g in range(8):
            far = levels[np.abs(levels - a[p, g]) >= 10]
            a[p, g + 8] = far[np.random.randint(len(far))]
    return np.exp2(a.ravel()).repeat(32)


def f64(x):
    return np.asarray(x).astype(np.float64)


def striped(idx):
    return np.tile(idx.reshape(-1, 16).T, (8, 1)).astype(np.uint16)


def unstriped(offs):
    return offs[:16].T.reshape(-1).astype(np.int64)


def pack_weight(w):
    k, n = w.shape
    w = f64(np.asarray(w, np.float32).astype(ml_dtypes.bfloat16)).reshape(k // 32, 32, n)
    amax = np.abs(w).max(1)
    byte = np.clip(np.where(amax > 0, np.frexp(amax)[1] - 1 + 127 - 7, 1), 1, 254)
    scaled = (w * np.exp2(127.0 - byte)[:, None, :]).reshape(k, n).astype(np.float32)
    words = np.ascontiguousarray(scaled.reshape(k // 512, 128, 4, n).transpose(0, 1, 3, 2)).astype(ml_dtypes.float8_e4m3fn).view(np.uint8)
    return words, np.ascontiguousarray(byte.astype(np.uint8).reshape(k // 512, 16, n))


def unpack_weight(words, scales):
    g, p, n, _ = words.shape
    vals = np.ascontiguousarray(words).view(ml_dtypes.float8_e4m3fn).astype(np.float64) * np.repeat(np.exp2(scales.astype(np.float64) - 127.0), 8, axis=1)[..., None]
    return vals.transpose(0, 1, 3, 2).reshape(g * 512, n)


E2M1 = np.array([0.0, 0.5, 1.0, 1.5, 2.0, 3.0, 4.0, 6.0, -0.0, -0.5, -1.0, -1.5, -2.0, -3.0, -4.0, -6.0])


def pack_fp4(w):
    k, n = w.shape
    w = f64(np.asarray(w, np.float32).astype(ml_dtypes.bfloat16)).reshape(k // 32, 32, n)
    amax = np.abs(w).max(1)
    mant, ex = np.frexp(amax / 6.0)
    byte = np.clip(np.where(amax > 0, np.where(mant > 0.5, ex, ex - 1) + 127, 1), 1, 254)
    scaled = (w * np.exp2(127.0 - byte)[:, None, :]).reshape(k, n).astype(np.float32)
    c = np.ascontiguousarray(scaled.reshape(k // 512, 128, 4, n).transpose(0, 1, 3, 2)).astype(ml_dtypes.float4_e2m1fn).view(np.uint8) & 0xF
    words = (c[..., 0::2] | (c[..., 1::2] << 4)).reshape(k // 512, 128, 2 * n)
    return np.ascontiguousarray(words), np.ascontiguousarray(byte.astype(np.uint8).reshape(k // 512, 16, n))


def unpack_fp4(words, scales):
    g, _, n = scales.shape
    words = np.ascontiguousarray(words).reshape(g, 128, n, 2)
    nib = np.empty((g, 128, n, 4), np.uint8)
    nib[..., 0::2] = words & 0xF
    nib[..., 1::2] = words >> 4
    vals = E2M1[nib] * np.repeat(np.exp2(scales.astype(np.float64) - 127.0), 8, axis=1)[..., None]
    return vals.transpose(0, 1, 3, 2).reshape(g * 512, n)


def sigmoid(v):
    return 1.0 / (1.0 + np.exp(-np.maximum(v, -700.0)))


K, T, S, D, N, H = 1024, 1024, 512, 4, 128, 512


def setup_inputs():
    n = np.random.standard_normal
    s = mx_kscale(K)[:, None]
    u = mx_kscale(H)
    packed_xT = pack_weight(n((K, T)) * s)
    packed_w1 = pack_fp4(n((K, H)) / np.sqrt(K) / s)
    packed_w2 = pack_fp4(n((K, H)) / np.sqrt(K) / s)
    packed_w3 = pack_fp4(n((H, N)) / np.sqrt(H) / u[:, None])
    return {
        "x_words": packed_xT[0],
        "x_scales": packed_xT[1],
        "w1_words": packed_w1[0],
        "w1_scales": packed_w1[1],
        "w2_words": packed_w2[0],
        "w2_scales": packed_w2[1],
        "ff": (np.random.uniform(0.05, 0.4, (H, S))).astype(np.float32),
        "unit": (np.random.uniform(0.6, 1.4, (H, 1)) * u[:, None]).astype(np.float32),
        "w3_words": packed_w3[0],
        "w3_scales": packed_w3[1],
        "offs": striped(np.random.permutation(T)[:S]),
        "see": striped(np.random.permutation(S)),
    }


def reference(x_words, x_scales, w1_words, w1_scales, w2_words, w2_scales, ff, unit, w3_words, w3_scales, offs, see):
    xq = unpack_weight(x_words, x_scales)[:, unstriped(offs)]
    em = unpack_fp4(w1_words, w1_scales).T @ xq
    emi = np.log(np.exp(em) + 1.0)
    rf = unpack_fp4(w2_words, w2_scales).T @ xq
    rho = 0.9 * sigmoid(rf)
    es = emi[:, unstriped(see)]
    ef = es * f64(ff)
    inc = ef.reshape(len(ef), -1, D).sum(axis=2)
    bone = emi + rho * np.repeat(inc, D, axis=1)
    bs = bone[:, unstriped(see)]
    bf = bs * f64(ff)
    inc2 = bf.reshape(len(bf), -1, D).sum(axis=2)
    dg = np.repeat(inc2, D, axis=1) - np.repeat(inc, D, axis=1)
    hid = f64(unit) * (dg * rho + bone)
    return unpack_fp4(w3_words, w3_scales).T @ mxq(hid, 0, "e4m3")

@@ -1,0 +1,248 @@
+from contextlib import ExitStack
+
+import concourse.mybir as mybir
+from concourse.masks import make_identity
+
+K, T, S, D, N, H = 1024, 1024, 512, 4, 128, 512
+FLOPS = 2 * (2 * K * H * S + H * N * S)
+
+F32 = mybir.dt.float32
+BF16 = mybir.dt.bfloat16
+I32 = mybir.dt.int32
+U32 = mybir.dt.uint32
+U16 = mybir.dt.uint16
+U8 = mybir.dt.uint8
+FP8X4 = mybir.dt.float8_e4m3fn_x4
+FP4X4 = mybir.dt.float4_e2m1fn_x4
+ALU = mybir.AluOpType
+ACT = mybir.ActivationFunctionType
+
+P = 128
+PACK = 4
+PASSES = K // (P * PACK)
+V = S // D
+SPARE = 8
+CLAMP = 30.0
+ALIGN = 64
+HALVES = 2
+FIRST_ON_SCALAR = (0, 1)
+SECOND_ON_SCALAR = (2, 0, 1)
+ORDER = (2, 0, 1, 3)
+ORDER2 = (2, 0, 3, 1)
+
+
+def tile_picked_yradio_chg_p_kernel(
+    tc, x_words, x_scales, w1_words, w1_scales, w2_words, w2_scales, ff, unit, w3_words, w3_scales, offs, see, out
+):
+    nc = tc.nc
+    with ExitStack() as ctx:
+        sb = ctx.enter_context(tc.tile_pool(name="sb", bufs=1))
+        ps = ctx.enter_context(tc.psum_pool(name="ps", bufs=1))
+
+        def tile(name, shape, dtype, tag=None):
+            return sb.tile(shape, dtype, name=name, tag=tag or name, align_bytes=ALIGN)
+
+        offs_t = sb.tile([P, S // 16], U16, name="offs_t")
+        see_t = sb.tile([P, S // 16], U16, name="see_t")
+        xs_win = tile("xs_win", [P, T], U8)
+        ws_stage = tile("ws_stage", [P, PASSES, H], U8)
+        ww_stage = tile("ww_stage", [P, PASSES, 2 * H], U8)
+        xs_late = tile("xs_late", [P, S], U8)
+        xw_win = [tile("xw_win%d" % g, [P, T], U32, tag="big%d" % g) for g in range(PASSES)]
+        unit_t = tile("unit_t", [P, PACK], F32)
+
+        nc.gpsimd.memset(xs_win[:].bitcast(I32), 0)
+        nc.gpsimd.memset(ws_stage[:].rearrange("p g n -> p (g n)").bitcast(I32), 0)
+        nc.gpsimd.memset(xs_late[:].bitcast(I32), 0)
+
+        def load_x_words(g):
+            nc.sync.dma_start(xw_win[g][:].bitcast(I32), x_words[g].rearrange("p n t -> p (n t)").bitcast(I32))
+
+        def load_w_words(words):
+            nc.sync.dma_start(ww_stage[:].bitcast(I32), words.rearrange("g p n -> p g n").bitcast(I32))
+
+        def load_w_scales(queue, scales):
+            for q in range(4):
+                queue.dma_start(
+                    ws_stage[32 * q : 32 * q + 4, :, :].bitcast(I32),
+                    scales[:, 4 * q : 4 * q + 4, :].rearrange("g r n -> r g n").bitcast(I32),
+                )
+
+        nc.sync.dma_start(offs_t[:], offs)
+        load_x_words(0)
+        for q in range(4):
+            nc.scalar.dma_start(
+                xs_win[32 * q : 32 * q + 8, :].bitcast(I32), x_scales[:, 4 * q : 4 * q + 4, :].bitcast(I32)
+            )
+        load_w_words(w1_words)
+        load_x_words(1)
+        load_w_scales(nc.scalar, w1_scales)
+        nc.sync.dma_start(see_t[:], see)
+
+        ident = tile("ident", [P, P], F32)
+        make_identity(nc, ident[:])
+        emi = [tile("emi%d" % t, [P, S + SPARE], F32) for t in range(PACK)]
+        lit = [tile("lit%d" % t, [P, S + SPARE], F32) for t in range(PACK)]
+        for win in emi + lit:
+            nc.gpsimd.memset(win[:, S:], 0.0)
+        nc.gpsimd.dma_start(unit_t[:], unit.rearrange("(p t) o -> p (t o)", t=PACK))
+        unit9 = tile("unit9", [P, PACK], F32)
+        nc.scalar.activation(unit9[:], unit_t[:], ACT.Copy, scale=0.9)
+
+        def deal(name):
+            words = tile(name + "_w", [P, PASSES, PACK, 2 * P], U8)
+            scales = tile(name + "_s", [P, PASSES, PACK, P], U8)
+            nc.vector.tensor_copy(
+                words[:].bitcast(U16),
+                ww_stage[:].bitcast(U16).rearrange("p g (m t) -> p g t m", t=PACK),
+            )
+            nc.vector.tensor_copy(scales[:], ws_stage[:].rearrange("p g (m t) -> p g t m", t=PACK))
+            return words, scales
+
+        xs_pick = tile("xs_pick", [P, S], U8)
+        nc.vector.tensor_copy(xs_pick[:], xs_win[:].indirect(offs_t[:]))
+        for q in range(4):
+            nc.sync.dma_start(
+                xs_late[32 * q : 32 * q + 4, :].bitcast(I32), xs_pick[32 * q + 4 : 32 * q + 8, :].bitcast(I32)
+            )
+        xs = [xs_pick, xs_late]
+        xw = [tile("xw%d" % g, [P, S], U32) for g in range(PASSES)]
+        nc.vector.tensor_copy(xw[0][:], xw_win[0][:].indirect(offs_t[:]))
+        w1 = deal("w1")
+        nc.vector.tensor_copy(xw[1][:], xw_win[1][:].indirect(offs_t[:]))
+
+        def product(banks, w):
+            for t in range(PACK):
+                for g in range(PASSES):
+                    nc.tensor.matmul_mx(
+                        out=banks[t][:],
+                        lhsT=w[0][:, g, t, :].bitcast(FP4X4),
+                        lhsT_scale=w[1][:, g, t, :],
+                        rhs=xw[g][:].bitcast(FP8X4),
+                        rhs_scale=xs[g][:],
+                        start=(g == 0),
+                        stop=(g == PASSES - 1),
+                    )
+
+        em = [ps.tile([P, S], F32, name="em%d" % t) for t in range(PACK)]
+        rf = [ps.tile([P, S], F32, name="rf%d" % t) for t in range(PACK)]
+        product(em, w1)
+
+        load_w_words(w2_words)
+        load_w_scales(nc.sync, w2_scales)
+        ff_view = ff.rearrange("(p t) s -> p t s", t=PACK)
+        ff_half = [tile("ff%d" % g, [P, 2, S], F32, tag="big%d" % g) for g in range(2)]
+        for g in range(2):
+            nc.sync.dma_start(ff_half[g][:], ff_view[:, 2 * g : 2 * g + 2, :])
+        fft = [ff_half[t // 2][:, t % 2, :] for t in range(PACK)]
+
+        logs = tile("logs", [P, PACK, S], F32)
+        sig = tile("sig", [P, PACK, S], F32)
+        last = PACK - 1
+        low = [tile("low%d" % t, [P, PACK, V], F32)[:] for t in range(last)] + [logs[:, :, 0:V]]
+        ex = [tile("ex%d" % t, [P, PACK, V], F32)[:] for t in range(last)] + [sig[:, :, 0:V]]
+        for t in range(PACK):
+            nc.vector.tensor_scalar_min(low[t], em[t][:].rearrange("p (a v) -> p a v", a=PACK), CLAMP)
+            nc.scalar.activation(ex[t], low[t], ACT.Exp)
+
+        w2 = deal("w2")
+        product(rf, w2)
+        nc.sync.dma_start(ww_stage[:, 0, 0 : 2 * N].bitcast(I32), w3_words[0].bitcast(I32))
+        for q in range(4):
+            nc.sync.dma_start(
+                ws_stage[32 * q : 32 * q + 4, 0, 0:N].bitcast(I32), w3_scales[0, 4 * q : 4 * q + 4, :].bitcast(I32)
+            )
+
+        for t in range(PACK):
+            nc.scalar.activation(logs[:, t, :].rearrange("p (a v) -> p a v", a=PACK), ex[t], ACT.Ln, bias=1.0)
+
+        def group_sums_turned(bank, cols, prod, name):
+            view = prod[:].rearrange("p (v d) -> p d v", d=D)
+            for d in range(D):
+                nc.tensor.matmul(
+                    bank[:, cols], view[:, d, :], ident[:], start=(d == 0), stop=(d == D - 1), is_transpose=True
+                )
+            turned = tile(name, [P, P], F32)
+            nc.scalar.copy(turned[:], bank[:, cols])
+            return turned
+
+        def turn_back(bank, cols, parts):
+            for i, part in enumerate(parts):
+                nc.tensor.matmul(
+                    bank[:, cols], part[:], ident[:], start=(i == 0), stop=(i == len(parts) - 1), is_transpose=True
+                )
+            return bank[:, cols].unsqueeze(2).to_broadcast([P, V, D])
+
+        def grouped(ap):
+            return ap.rearrange("p (v d) -> p v d", d=D)
+
+        def seen_times_ff(win, t, on_scalar, name):
+            prod = tile(name, [P, S], F32)
+            if on_scalar is not None:
+                nc.vector.tensor_tensor(prod[:], on_scalar[:], fft[t], ALU.mult)
+            else:
+                nc.vector.tensor_tensor(prod[:], win[:].indirect(see_t[:]), fft[t], ALU.mult)
+            return prod
+
+        def scalar_gather(win, name):
+            seen = tile(name, [P, S], F32)
+            nc.scalar.activation(seen[:], win[:].indirect(see_t[:]), ACT.Copy)
+            return seen
+
+        for t in range(PACK):
+            nc.vector.tensor_tensor(emi[t][:, 0:S], logs[:, t, :], em[t][:], ALU.max)
+        seen = {t: scalar_gather(emi[t], "es%d" % t) for t in FIRST_ON_SCALAR}
+        inc_turned = {}
+        inc = {}
+        for t in ORDER:
+            ef = seen_times_ff(emi[t], t, seen.get(t), "ef%d" % t)
+            inc_turned[t] = group_sums_turned(em[t], slice(0, V), ef, "inc_turned%d" % t)
+            inc[t] = turn_back(em[t], slice(V, 2 * V), [inc_turned[t]])
+
+        for t in ORDER:
+            nc.scalar.activation(sig[:, t, :], rf[t][:], ACT.Sigmoid)
+
+        for t in ORDER:
+            nc.vector.scalar_tensor_tensor(grouped(lit[t][:, 0:S]), inc[t], 0.9, grouped(sig[:, t, :]), ALU.mult, ALU.mult)
+        seen = {t: scalar_gather(lit[t], "bs%d" % t) for t in SECOND_ON_SCALAR}
+        inc2 = {}
+        for t in ORDER2:
+            bf = seen_times_ff(lit[t], t, seen.get(t), "bf%d" % t)
+            dg_turned = group_sums_turned(em[t], slice(2 * V, 3 * V), bf, "dg_turned%d" % t)
+            inc2[t] = turn_back(em[t], slice(3 * V, 4 * V), [inc_turned[t], dg_turned])
+
+        planes = tile("planes", [P, PACK, S], BF16)
+        for t in ORDER2:
+            back = tile("back%d" % t, [P, S], F32)
+            nc.vector.scalar_tensor_tensor(
+                grouped(back[:]), inc2[t], unit9[:, t : t + 1], grouped(sig[:, t, :]), ALU.mult, ALU.mult
+            )
+            nc.vector.scalar_tensor_tensor(
+                planes[:, t, :], emi[t][:, 0:S], unit_t[:, t : t + 1], back[:], ALU.mult, ALU.add
+            )
+
+        width = S // HALVES
+        woven = [tile("woven%d" % h, [P, width, PACK], BF16) for h in range(HALVES)]
+        for h in range(HALVES):
+            nc.vector.tensor_copy(
+                woven[h][:].rearrange("p (c i) t -> p c t i", i=4),
+                planes[:, :, h * width : (h + 1) * width].rearrange("p t (c i) -> p c t i", i=4),
+            )
+        for h in range(HALVES):
+            codes = tile("codes%d" % h, [P, width], U32)
+            plane = tile("plane%d" % h, [P, width], U8)
+            nc.vector.quantize_mx(
+                out=codes[:].bitcast(FP8X4), scales=plane[:], in_=woven[h][:].rearrange("p j t -> p (j t)")
+            )
+            nc.tensor.matmul_mx(
+                out=rf[h][:, 0:width],
+                lhsT=ww_stage[:, 0, 0 : 2 * N].bitcast(FP4X4),
+                lhsT_scale=ws_stage[:, 0, 0:N],
+                rhs=codes[:].bitcast(FP8X4),
+                rhs_scale=plane[:],
+                start=True,
+                stop=True,
+            )
+            result = tile("result%d" % h, [P, width], F32)
+            nc.scalar.copy(result[:], rf[h][:, 0:width])
+            nc.sync.dma_start(out[:, h * width : (h + 1) * width], result[:])

@@ -21,14 +21,10 @@ P = 128
 PACK = 4
 PASSES = K // (P * PACK)
 V = S // D
-SPARE = 8
-CLAMP = 30.0
+TINY = 2.0**-60
 ALIGN = 64
 HALVES = 2
-FIRST_ON_SCALAR = (0, 1)
-SECOND_ON_SCALAR = (2, 0, 1)
-ORDER = (2, 0, 1, 3)
-ORDER2 = (2, 0, 3, 1)
+FIRST_LAST = (1, 2, 3, 0)
 
 
 def tile_picked_yradio_chg_p_kernel(
@@ -58,66 +54,67 @@ def tile_picked_yradio_chg_p_kernel(
         def load_x_words(g):
             nc.sync.dma_start(xw_win[g][:].bitcast(I32), x_words[g].rearrange("p n t -> p (n t)").bitcast(I32))
 
-        def load_w_words(words):
-            nc.sync.dma_start(ww_stage[:].bitcast(I32), words.rearrange("g p n -> p g n").bitcast(I32))
+        def load_w_words(queue, words):
+            queue.dma_start(ww_stage[:].bitcast(I32), words.rearrange("g p n -> p g n").bitcast(I32))
 
-        def load_w_scales(queue, scales):
-            for q in range(4):
-                queue.dma_start(
-                    ws_stage[32 * q : 32 * q + 4, :, :].bitcast(I32),
-                    scales[:, 4 * q : 4 * q + 4, :].rearrange("g r n -> r g n").bitcast(I32),
-                )
+        def load_w_scales(queue, scales, q):
+            queue.dma_start(
+                ws_stage[32 * q : 32 * q + 4, :, :].bitcast(I32),
+                scales[:, 4 * q : 4 * q + 4, :].rearrange("g r n -> r g n").bitcast(I32),
+            )
 
         nc.sync.dma_start(offs_t[:], offs)
-        load_x_words(0)
+        load_w_words(nc.scalar, w1_words)
         for q in range(4):
-            nc.scalar.dma_start(
+            (nc.sync if q < 2 else nc.scalar).dma_start(
                 xs_win[32 * q : 32 * q + 8, :].bitcast(I32), x_scales[:, 4 * q : 4 * q + 4, :].bitcast(I32)
             )
-        load_w_words(w1_words)
-        load_x_words(1)
-        load_w_scales(nc.scalar, w1_scales)
+        load_x_words(0)
+        for q in range(4):
+            load_w_scales(nc.sync if q == 0 else nc.scalar, w1_scales, q)
         nc.sync.dma_start(see_t[:], see)
+        load_x_words(1)
 
         ident = tile("ident", [P, P], F32)
         make_identity(nc, ident[:])
-        emi = [tile("emi%d" % t, [P, S + SPARE], F32) for t in range(PACK)]
-        lit = [tile("lit%d" % t, [P, S + SPARE], F32) for t in range(PACK)]
-        for win in emi + lit:
-            nc.gpsimd.memset(win[:, S:], 0.0)
+        emi = [tile("emi%d" % t, [P, 2 * S], F32) for t in range(PACK)]
+        lit = [tile("lit%d" % t, [P, 2 * S], F32) for t in range(PACK)]
         nc.gpsimd.dma_start(unit_t[:], unit.rearrange("(p t) o -> p (t o)", t=PACK))
-        unit9 = tile("unit9", [P, PACK], F32)
-        nc.scalar.activation(unit9[:], unit_t[:], ACT.Copy, scale=0.9)
 
-        def deal(name):
-            words = tile(name + "_w", [P, PASSES, PACK, 2 * P], U8)
-            scales = tile(name + "_s", [P, PASSES, PACK, P], U8)
+        def deal_words(name):
+            words = tile(name, [P, PASSES, PACK, 2 * P], U8)
             nc.vector.tensor_copy(
-                words[:].bitcast(U16),
-                ww_stage[:].bitcast(U16).rearrange("p g (m t) -> p g t m", t=PACK),
+                words[:].bitcast(U16), ww_stage[:].bitcast(U16).rearrange("p g (m t) -> p g t m", t=PACK)
             )
-            nc.vector.tensor_copy(scales[:], ws_stage[:].rearrange("p g (m t) -> p g t m", t=PACK))
-            return words, scales
+            return words
 
+        def deal_scales(name, tiles, tag=None):
+            scales = tile(name, [P, PASSES, len(tiles), P], U8, tag=tag)
+            dealt = ws_stage[:].rearrange("p g (m t) -> p g t m", t=PACK)
+            nc.vector.tensor_copy(scales[:], dealt[:, :, tiles[0] : tiles[-1] + 1 : tiles[1] - tiles[0], :])
+            return {t: scales[:, :, i, :] for i, t in enumerate(tiles)}
+
+        w1_dealt = deal_words("w1_dealt")
         xs_pick = tile("xs_pick", [P, S], U8)
         nc.vector.tensor_copy(xs_pick[:], xs_win[:].indirect(offs_t[:]))
         for q in range(4):
-            nc.sync.dma_start(
+            (nc.sync if q < 2 else nc.scalar).dma_start(
                 xs_late[32 * q : 32 * q + 4, :].bitcast(I32), xs_pick[32 * q + 4 : 32 * q + 8, :].bitcast(I32)
             )
         xs = [xs_pick, xs_late]
         xw = [tile("xw%d" % g, [P, S], U32) for g in range(PASSES)]
         nc.vector.tensor_copy(xw[0][:], xw_win[0][:].indirect(offs_t[:]))
-        w1 = deal("w1")
+        w1_planes = deal_scales("w1_early", (1, 2))
         nc.vector.tensor_copy(xw[1][:], xw_win[1][:].indirect(offs_t[:]))
+        w1_planes = {**w1_planes, **deal_scales("w1_late", (0, 3), tag="big1")}
 
-        def product(banks, w):
-            for t in range(PACK):
+        def product(banks, words, planes, order):
+            for t in order:
                 for g in range(PASSES):
                     nc.tensor.matmul_mx(
                         out=banks[t][:],
-                        lhsT=w[0][:, g, t, :].bitcast(FP4X4),
-                        lhsT_scale=w[1][:, g, t, :],
+                        lhsT=words[:, g, t, :].bitcast(FP4X4),
+                        lhsT_scale=planes[t][:, g, :],
                         rhs=xw[g][:].bitcast(FP8X4),
                         rhs_scale=xs[g][:],
                         start=(g == 0),
@@ -126,27 +123,30 @@ def tile_picked_yradio_chg_p_kernel(
 
         em = [ps.tile([P, S], F32, name="em%d" % t) for t in range(PACK)]
         rf = [ps.tile([P, S], F32, name="rf%d" % t) for t in range(PACK)]
-        product(em, w1)
+        product(em, w1_dealt, w1_planes, FIRST_LAST)
 
-        load_w_words(w2_words)
-        load_w_scales(nc.sync, w2_scales)
+        load_w_words(nc.sync, w2_words)
+        for q in range(4):
+            load_w_scales(nc.sync, w2_scales, q)
         ff_view = ff.rearrange("(p t) s -> p t s", t=PACK)
         ff_half = [tile("ff%d" % g, [P, 2, S], F32, tag="big%d" % g) for g in range(2)]
         for g in range(2):
             nc.sync.dma_start(ff_half[g][:], ff_view[:, 2 * g : 2 * g + 2, :])
         fft = [ff_half[t // 2][:, t % 2, :] for t in range(PACK)]
 
-        logs = tile("logs", [P, PACK, S], F32)
-        sig = tile("sig", [P, PACK, S], F32)
-        last = PACK - 1
-        low = [tile("low%d" % t, [P, PACK, V], F32)[:] for t in range(last)] + [logs[:, :, 0:V]]
-        ex = [tile("ex%d" % t, [P, PACK, V], F32)[:] for t in range(last)] + [sig[:, :, 0:V]]
-        for t in range(PACK):
-            nc.vector.tensor_scalar_min(low[t], em[t][:].rearrange("p (a v) -> p a v", a=PACK), CLAMP)
-            nc.scalar.activation(ex[t], low[t], ACT.Exp)
+        log_rows = tile("log_rows", [P, PACK, S], F32)
 
-        w2 = deal("w2")
-        product(rf, w2)
+        def quarters(ap):
+            return ap.rearrange("p (a v) -> p a v", a=PACK)
+
+        side = [emi[t][:, S:] for t in range(PACK)]
+        fall = [log_rows[:, :, 0:V]] + [quarters(side[t]) for t in range(1, PACK)]
+        logs = [side[0]] + [log_rows[:, t, :] for t in range(1, PACK)]
+        for t in FIRST_LAST:
+            nc.scalar.activation(fall[t], quarters(em[t][:]), ACT.Sigmoid, scale=-1.0)
+
+        w2_planes = deal_scales("w2_planes", tuple(range(PACK)))
+        product(rf, deal_words("w2_dealt"), w2_planes, range(PACK))
         nc.sync.dma_start(ww_stage[:, 0, 0 : 2 * N].bitcast(I32), w3_words[0].bitcast(I32))
         for q in range(4):
             nc.sync.dma_start(
@@ -154,16 +154,15 @@ def tile_picked_yradio_chg_p_kernel(
             )
 
         for t in range(PACK):
-            nc.scalar.activation(logs[:, t, :].rearrange("p (a v) -> p a v", a=PACK), ex[t], ACT.Ln, bias=1.0)
+            nc.scalar.activation(quarters(logs[t]), fall[t], ACT.Ln, bias=TINY)
 
-        def group_sums_turned(bank, cols, prod, name):
-            view = prod[:].rearrange("p (v d) -> p d v", d=D)
+        def group_sums_turned(bank, cols, members, name):
             for d in range(D):
                 nc.tensor.matmul(
-                    bank[:, cols], view[:, d, :], ident[:], start=(d == 0), stop=(d == D - 1), is_transpose=True
+                    bank[:, cols], members[:, d, :], ident[:], start=(d == 0), stop=(d == D - 1), is_transpose=True
                 )
             turned = tile(name, [P, P], F32)
-            nc.scalar.copy(turned[:], bank[:, cols])
+            nc.scalar.activation(turned[:], bank[:, cols], ACT.Copy, scale=0.9)
             return turned
 
         def turn_back(bank, cols, parts):
@@ -176,46 +175,60 @@ def tile_picked_yradio_chg_p_kernel(
         def grouped(ap):
             return ap.rearrange("p (v d) -> p v d", d=D)
 
-        def seen_times_ff(win, t, on_scalar, name):
-            prod = tile(name, [P, S], F32)
-            if on_scalar is not None:
-                nc.vector.tensor_tensor(prod[:], on_scalar[:], fft[t], ALU.mult)
-            else:
-                nc.vector.tensor_tensor(prod[:], win[:].indirect(see_t[:]), fft[t], ALU.mult)
-            return prod
-
         def scalar_gather(win, name):
             seen = tile(name, [P, S], F32)
             nc.scalar.activation(seen[:], win[:].indirect(see_t[:]), ACT.Copy)
             return seen
 
-        for t in range(PACK):
-            nc.vector.tensor_tensor(emi[t][:, 0:S], logs[:, t, :], em[t][:], ALU.max)
-        seen = {t: scalar_gather(emi[t], "es%d" % t) for t in FIRST_ON_SCALAR}
+        def times_ff(prod, win, t, seen):
+            if seen is None:
+                nc.vector.tensor_tensor(prod, win[:].indirect(see_t[:]), fft[t], ALU.mult)
+                return prod.rearrange("p (v d) -> p d v", d=D)
+            nc.vector.tensor_tensor(prod.rearrange("p (d v) -> p v d", d=D), grouped(seen[:]), grouped(fft[t]), ALU.mult)
+            return prod.rearrange("p (d v) -> p d v", d=D)
+
         inc_turned = {}
         inc = {}
-        for t in ORDER:
-            ef = seen_times_ff(emi[t], t, seen.get(t), "ef%d" % t)
-            inc_turned[t] = group_sums_turned(em[t], slice(0, V), ef, "inc_turned%d" % t)
+        inc2 = {}
+
+        def emission(t):
+            nc.vector.scalar_tensor_tensor(emi[t][:, 0:S], logs[t], -1.0, em[t][:], ALU.mult, ALU.max)
+
+        def first_bounce(t, seen):
+            members = times_ff(lit[t][:, S:], emi[t], t, seen)
+            inc_turned[t] = group_sums_turned(em[t], slice(0, V), members, "inc_turned%d" % t)
             inc[t] = turn_back(em[t], slice(V, 2 * V), [inc_turned[t]])
 
-        for t in ORDER:
-            nc.scalar.activation(sig[:, t, :], rf[t][:], ACT.Sigmoid)
-
-        for t in ORDER:
-            nc.vector.scalar_tensor_tensor(grouped(lit[t][:, 0:S]), inc[t], 0.9, grouped(sig[:, t, :]), ALU.mult, ALU.mult)
-        seen = {t: scalar_gather(lit[t], "bs%d" % t) for t in SECOND_ON_SCALAR}
-        inc2 = {}
-        for t in ORDER2:
-            bf = seen_times_ff(lit[t], t, seen.get(t), "bf%d" % t)
-            dg_turned = group_sums_turned(em[t], slice(2 * V, 3 * V), bf, "dg_turned%d" % t)
+        def second_bounce(t, seen):
+            bf = tile("bf%d" % t, [P, S], F32)
+            members = times_ff(bf[:], lit[t], t, seen)
+            dg_turned = group_sums_turned(em[t], slice(2 * V, 3 * V), members, "dg_turned%d" % t)
             inc2[t] = turn_back(em[t], slice(3 * V, 4 * V), [inc_turned[t], dg_turned])
 
+        emission(0)
+        es = scalar_gather(emi[0], "es")
+        for t in range(1, PACK):
+            emission(t)
+            first_bounce(t, None)
+            if t == 1:
+                first_bounce(0, es)
+
+        seen = {}
+        for t in range(PACK):
+            nc.scalar.activation(side[t], rf[t][:], ACT.Sigmoid)
+            nc.vector.tensor_tensor(grouped(lit[t][:, 0:S]), inc[t], grouped(side[t]), ALU.mult)
+            if t % 2 == 0:
+                seen[t] = scalar_gather(lit[t], "seen%d" % t)
+            else:
+                second_bounce(t, None)
+        for t in range(0, PACK, 2):
+            second_bounce(t, seen[t])
+
         planes = tile("planes", [P, PACK, S], BF16)
-        for t in ORDER2:
+        for t in range(PACK):
             back = tile("back%d" % t, [P, S], F32)
             nc.vector.scalar_tensor_tensor(
-                grouped(back[:]), inc2[t], unit9[:, t : t + 1], grouped(sig[:, t, :]), ALU.mult, ALU.mult
+                grouped(back[:]), inc2[t], unit_t[:, t : t + 1], grouped(side[t]), ALU.mult, ALU.mult
             )
             nc.vector.scalar_tensor_tensor(
                 planes[:, t, :], emi[t][:, 0:S], unit_t[:, t : t + 1], back[:], ALU.mult, ALU.add

from contextlib import ExitStack

import concourse.mybir as mybir
from concourse.masks import make_identity

K, T, S, D, N, H = 1024, 1024, 512, 4, 128, 512
FLOPS = 2 * (2 * K * H * S + H * N * S)

F32 = mybir.dt.float32
BF16 = mybir.dt.bfloat16
I32 = mybir.dt.int32
U32 = mybir.dt.uint32
U16 = mybir.dt.uint16
U8 = mybir.dt.uint8
FP8X4 = mybir.dt.float8_e4m3fn_x4
FP4X4 = mybir.dt.float4_e2m1fn_x4
ALU = mybir.AluOpType
ACT = mybir.ActivationFunctionType

P = 128
PACK = 4
PASSES = K // (P * PACK)
V = S // D
TINY = 2.0**-60
ALIGN = 64
HALVES = 2
FIRST_LAST = (1, 2, 3, 0)


def tile_picked_yradio_chg_p_kernel(
    tc, x_words, x_scales, w1_words, w1_scales, w2_words, w2_scales, ff, unit, w3_words, w3_scales, offs, see, out
):
    nc = tc.nc
    with ExitStack() as ctx:
        sb = ctx.enter_context(tc.tile_pool(name="sb", bufs=1))
        ps = ctx.enter_context(tc.psum_pool(name="ps", bufs=1))

        def tile(name, shape, dtype, tag=None):
            return sb.tile(shape, dtype, name=name, tag=tag or name, align_bytes=ALIGN)

        offs_t = sb.tile([P, S // 16], U16, name="offs_t")
        see_t = sb.tile([P, S // 16], U16, name="see_t")
        xs_win = tile("xs_win", [P, T], U8)
        ws_stage = tile("ws_stage", [P, PASSES, H], U8)
        ww_stage = tile("ww_stage", [P, PASSES, 2 * H], U8)
        xs_late = tile("xs_late", [P, S], U8)
        xw_win = [tile("xw_win%d" % g, [P, T], U32, tag="big%d" % g) for g in range(PASSES)]
        unit_t = tile("unit_t", [P, PACK], F32)

        nc.gpsimd.memset(xs_win[:].bitcast(I32), 0)
        nc.gpsimd.memset(ws_stage[:].rearrange("p g n -> p (g n)").bitcast(I32), 0)
        nc.gpsimd.memset(xs_late[:].bitcast(I32), 0)

        def load_x_words(g):
            nc.sync.dma_start(xw_win[g][:].bitcast(I32), x_words[g].rearrange("p n t -> p (n t)").bitcast(I32))

        def load_w_words(queue, words):
            queue.dma_start(ww_stage[:].bitcast(I32), words.rearrange("g p n -> p g n").bitcast(I32))

        def load_w_scales(queue, scales, q):
            queue.dma_start(
                ws_stage[32 * q : 32 * q + 4, :, :].bitcast(I32),
                scales[:, 4 * q : 4 * q + 4, :].rearrange("g r n -> r g n").bitcast(I32),
            )

        nc.sync.dma_start(offs_t[:], offs)
        load_w_words(nc.scalar, w1_words)
        for q in range(4):
            (nc.sync if q < 2 else nc.scalar).dma_start(
                xs_win[32 * q : 32 * q + 8, :].bitcast(I32), x_scales[:, 4 * q : 4 * q + 4, :].bitcast(I32)
            )
        load_x_words(0)
        for q in range(4):
            load_w_scales(nc.sync if q == 0 else nc.scalar, w1_scales, q)
        nc.sync.dma_start(see_t[:], see)
        load_x_words(1)

        ident = tile("ident", [P, P], F32)
        make_identity(nc, ident[:])
        emi = [tile("emi%d" % t, [P, 2 * S], F32) for t in range(PACK)]
        lit = [tile("lit%d" % t, [P, 2 * S], F32) for t in range(PACK)]
        nc.gpsimd.dma_start(unit_t[:], unit.rearrange("(p t) o -> p (t o)", t=PACK))

        def deal_words(name):
            words = tile(name, [P, PASSES, PACK, 2 * P], U8)
            nc.vector.tensor_copy(
                words[:].bitcast(U16), ww_stage[:].bitcast(U16).rearrange("p g (m t) -> p g t m", t=PACK)
            )
            return words

        def deal_scales(name, tiles, tag=None):
            scales = tile(name, [P, PASSES, len(tiles), P], U8, tag=tag)
            dealt = ws_stage[:].rearrange("p g (m t) -> p g t m", t=PACK)
            nc.vector.tensor_copy(scales[:], dealt[:, :, tiles[0] : tiles[-1] + 1 : tiles[1] - tiles[0], :])
            return {t: scales[:, :, i, :] for i, t in enumerate(tiles)}

        w1_dealt = deal_words("w1_dealt")
        xs_pick = tile("xs_pick", [P, S], U8)
        nc.vector.tensor_copy(xs_pick[:], xs_win[:].indirect(offs_t[:]))
        for q in range(4):
            (nc.sync if q < 2 else nc.scalar).dma_start(
                xs_late[32 * q : 32 * q + 4, :].bitcast(I32), xs_pick[32 * q + 4 : 32 * q + 8, :].bitcast(I32)
            )
        xs = [xs_pick, xs_late]
        xw = [tile("xw%d" % g, [P, S], U32) for g in range(PASSES)]
        nc.vector.tensor_copy(xw[0][:], xw_win[0][:].indirect(offs_t[:]))
        w1_planes = deal_scales("w1_early", (1, 2))
        nc.vector.tensor_copy(xw[1][:], xw_win[1][:].indirect(offs_t[:]))
        w1_planes = {**w1_planes, **deal_scales("w1_late", (0, 3), tag="big1")}

        def product(banks, words, planes, order):
            for t in order:
                for g in range(PASSES):
                    nc.tensor.matmul_mx(
                        out=banks[t][:],
                        lhsT=words[:, g, t, :].bitcast(FP4X4),
                        lhsT_scale=planes[t][:, g, :],
                        rhs=xw[g][:].bitcast(FP8X4),
                        rhs_scale=xs[g][:],
                        start=(g == 0),
                        stop=(g == PASSES - 1),
                    )

        em = [ps.tile([P, S], F32, name="em%d" % t) for t in range(PACK)]
        rf = [ps.tile([P, S], F32, name="rf%d" % t) for t in range(PACK)]
        product(em, w1_dealt, w1_planes, FIRST_LAST)

        load_w_words(nc.sync, w2_words)
        for q in range(4):
            load_w_scales(nc.sync, w2_scales, q)
        ff_view = ff.rearrange("(p t) s -> p t s", t=PACK)
        ff_half = [tile("ff%d" % g, [P, 2, S], F32, tag="big%d" % g) for g in range(2)]
        for g in range(2):
            nc.sync.dma_start(ff_half[g][:], ff_view[:, 2 * g : 2 * g + 2, :])
        fft = [ff_half[t // 2][:, t % 2, :] for t in range(PACK)]

        log_rows = tile("log_rows", [P, PACK, S], F32)

        def quarters(ap):
            return ap.rearrange("p (a v) -> p a v", a=PACK)

        side = [emi[t][:, S:] for t in range(PACK)]
        fall = [log_rows[:, :, 0:V]] + [quarters(side[t]) for t in range(1, PACK)]
        logs = [side[0]] + [log_rows[:, t, :] for t in range(1, PACK)]
        for t in FIRST_LAST:
            nc.scalar.activation(fall[t], quarters(em[t][:]), ACT.Sigmoid, scale=-1.0)

        w2_planes = deal_scales("w2_planes", tuple(range(PACK)))
        product(rf, deal_words("w2_dealt"), w2_planes, range(PACK))
        nc.sync.dma_start(ww_stage[:, 0, 0 : 2 * N].bitcast(I32), w3_words[0].bitcast(I32))
        for q in range(4):
            nc.sync.dma_start(
                ws_stage[32 * q : 32 * q + 4, 0, 0:N].bitcast(I32), w3_scales[0, 4 * q : 4 * q + 4, :].bitcast(I32)
            )

        for t in range(PACK):
            nc.scalar.activation(quarters(logs[t]), fall[t], ACT.Ln, bias=TINY)

        def group_sums_turned(bank, cols, members, name):
            for d in range(D):
                nc.tensor.matmul(
                    bank[:, cols], members[:, d, :], ident[:], start=(d == 0), stop=(d == D - 1), is_transpose=True
                )
            turned = tile(name, [P, P], F32)
            nc.scalar.activation(turned[:], bank[:, cols], ACT.Copy, scale=0.9)
            return turned

        def turn_back(bank, cols, parts):
            for i, part in enumerate(parts):
                nc.tensor.matmul(
                    bank[:, cols], part[:], ident[:], start=(i == 0), stop=(i == len(parts) - 1), is_transpose=True
                )
            return bank[:, cols].unsqueeze(2).to_broadcast([P, V, D])

        def grouped(ap):
            return ap.rearrange("p (v d) -> p v d", d=D)

        def scalar_gather(win, name):
            seen = tile(name, [P, S], F32)
            nc.scalar.activation(seen[:], win[:].indirect(see_t[:]), ACT.Copy)
            return seen

        def times_ff(prod, win, t, seen):
            if seen is None:
                nc.vector.tensor_tensor(prod, win[:].indirect(see_t[:]), fft[t], ALU.mult)
                return prod.rearrange("p (v d) -> p d v", d=D)
            nc.vector.tensor_tensor(prod.rearrange("p (d v) -> p v d", d=D), grouped(seen[:]), grouped(fft[t]), ALU.mult)
            return prod.rearrange("p (d v) -> p d v", d=D)

        inc_turned = {}
        inc = {}
        inc2 = {}

        def emission(t):
            nc.vector.scalar_tensor_tensor(emi[t][:, 0:S], logs[t], -1.0, em[t][:], ALU.mult, ALU.max)

        def first_bounce(t, seen):
            members = times_ff(lit[t][:, S:], emi[t], t, seen)
            inc_turned[t] = group_sums_turned(em[t], slice(0, V), members, "inc_turned%d" % t)
            inc[t] = turn_back(em[t], slice(V, 2 * V), [inc_turned[t]])

        def second_bounce(t, seen):
            bf = tile("bf%d" % t, [P, S], F32)
            members = times_ff(bf[:], lit[t], t, seen)
            dg_turned = group_sums_turned(em[t], slice(2 * V, 3 * V), members, "dg_turned%d" % t)
            inc2[t] = turn_back(em[t], slice(3 * V, 4 * V), [inc_turned[t], dg_turned])

        emission(0)
        es = scalar_gather(emi[0], "es")
        for t in range(1, PACK):
            emission(t)
            first_bounce(t, None)
            if t == 1:
                first_bounce(0, es)

        seen = {}
        for t in range(PACK):
            nc.scalar.activation(side[t], rf[t][:], ACT.Sigmoid)
            nc.vector.tensor_tensor(grouped(lit[t][:, 0:S]), inc[t], grouped(side[t]), ALU.mult)
            if t % 2 == 0:
                seen[t] = scalar_gather(lit[t], "seen%d" % t)
            else:
                second_bounce(t, None)
        for t in range(0, PACK, 2):
            second_bounce(t, seen[t])

        planes = tile("planes", [P, PACK, S], BF16)
        for t in range(PACK):
            back = tile("back%d" % t, [P, S], F32)
            nc.vector.scalar_tensor_tensor(
                grouped(back[:]), inc2[t], unit_t[:, t : t + 1], grouped(side[t]), ALU.mult, ALU.mult
            )
            nc.vector.scalar_tensor_tensor(
                planes[:, t, :], emi[t][:, 0:S], unit_t[:, t : t + 1], back[:], ALU.mult, ALU.add
            )

        width = S // HALVES
        woven = [tile("woven%d" % h, [P, width, PACK], BF16) for h in range(HALVES)]
        for h in range(HALVES):
            nc.vector.tensor_copy(
                woven[h][:].rearrange("p (c i) t -> p c t i", i=4),
                planes[:, :, h * width : (h + 1) * width].rearrange("p t (c i) -> p c t i", i=4),
            )
        for h in range(HALVES):
            codes = tile("codes%d" % h, [P, width], U32)
            plane = tile("plane%d" % h, [P, width], U8)
            nc.vector.quantize_mx(
                out=codes[:].bitcast(FP8X4), scales=plane[:], in_=woven[h][:].rearrange("p j t -> p (j t)")
            )
            nc.tensor.matmul_mx(
                out=rf[h][:, 0:width],
                lhsT=ww_stage[:, 0, 0 : 2 * N].bitcast(FP4X4),
                lhsT_scale=ws_stage[:, 0, 0:N],
                rhs=codes[:].bitcast(FP8X4),
                rhs_scale=plane[:],
                start=True,
                stop=True,
            )
            result = tile("result%d" % h, [P, width], F32)
            nc.scalar.copy(result[:], rf[h][:, 0:width])
            nc.sync.dma_start(out[:, h * width : (h + 1) * width], result[:])
